import numpy as np
import ml_dtypes


def mxq(x, axis, fmt="e4m3"):
    dtype, down = {"e4m3": (ml_dtypes.float8_e4m3fn, 7), "e5m2": (ml_dtypes.float8_e5m2, 14)}[fmt]
    v = np.moveaxis(np.asarray(x, np.float32).astype(ml_dtypes.bfloat16).astype(np.float64), axis, -1)
    blocks = v.reshape(v.shape[:-1] + (-1, 32))
    amax = np.abs(blocks).max(-1, keepdims=True)
    byte = np.maximum(np.where(amax > 0, np.frexp(amax)[1] - 1 + 127, 0) - down, 1)
    scale = np.exp2(byte - 127.0)
    codes = (blocks / scale).astype(np.float32).astype(dtype).astype(np.float64)
    return np.moveaxis((codes * scale).reshape(v.shape), -1, axis)


WIDE = False


def mx_kscale(k):
    if not WIDE:
        return np.ones(k)
    levels = np.array([10, -10, 5, -5, 0])
    if k % 512:
        return np.exp2(np.random.permutation(np.resize(levels, k // 32))).repeat(32)
    a = np.empty((k // 512, 16))
    for p in range(k // 512):
        a[p, :8] = np.random.permutation(np.resize(levels, 8))
        for g in range(8):
            far = levels[np.abs(levels - a[p, g]) >= 10]
            a[p, g + 8] = far[np.random.randint(len(far))]
    return np.exp2(a.ravel()).repeat(32)


def f64(x):
    return np.asarray(x).astype(np.float64)


def striped(idx):
    return np.tile(idx.reshape(-1, 16).T, (8, 1)).astype(np.uint16)


def unstriped(offs):
    return offs[:16].T.reshape(-1).astype(np.int64)


def striped8(idx):
    return np.concatenate([x.reshape(-1, 16).T for x in idx]).astype(np.uint16)


def runs(offs, k):
    lists = np.stack([offs[16 * r : 16 * r + 16].T.reshape(-1) for r in range(8)]).astype(np.int64)
    return lists[np.arange(k) % 512 // 64]


def pack_weight(w):
    k, n = w.shape
    w = f64(np.asarray(w, np.float32).astype(ml_dtypes.bfloat16)).reshape(k // 32, 32, n)
    amax = np.abs(w).max(1)
    byte = np.clip(np.where(amax > 0, np.frexp(amax)[1] - 1 + 127 - 7, 1), 1, 254)
    scaled = (w * np.exp2(127.0 - byte)[:, None, :]).reshape(k, n).astype(np.float32)
    words = np.ascontiguousarray(scaled.reshape(k // 512, 128, 4, n).transpose(0, 1, 3, 2)).astype(ml_dtypes.float8_e4m3fn).view(np.uint8)
    return words, np.ascontiguousarray(byte.astype(np.uint8).reshape(k // 512, 16, n))


def unpack_weight(words, scales):
    g, p, n, _ = words.shape
    vals = np.ascontiguousarray(words).view(ml_dtypes.float8_e4m3fn).astype(np.float64) * np.repeat(np.exp2(scales.astype(np.float64) - 127.0), 8, axis=1)[..., None]
    return vals.transpose(0, 1, 3, 2).reshape(g * 512, n)


def sigmoid(v):
    return 1.0 / (1.0 + np.exp(-np.maximum(v, -700.0)))

def planes(y):
    n, m = y.shape
    v = y.astype(np.float32).astype(ml_dtypes.bfloat16).astype(np.float64).reshape(n // 32, 32, m)
    top = np.abs(v).max(1)
    byte = np.clip(np.where(top > 0, np.frexp(top)[1] - 1 + 127 - 7, 1), 1, 254)
    codes = (v * np.exp2(127.0 - byte)[:, None, :]).reshape(n, m).astype(np.float32).astype(ml_dtypes.float8_e4m3fn).view(np.uint8)
    words = codes.reshape(n // 512, 128, 4, m).transpose(0, 1, 3, 2)
    return np.ascontiguousarray(words), np.ascontiguousarray(byte.astype(np.uint8).reshape(n // 512, 16, m))


K, T, S, N, H = 512, 2048, 512, 512, 512


def setup_inputs():
    n = np.random.standard_normal
    s = mx_kscale(K)[:, None]
    u = mx_kscale(H)
    packed_xT = pack_weight(n((K, T)) * s)
    packed_w1 = pack_weight(n((K, H)) / np.sqrt(K) / s)
    packed_w2 = pack_weight(n((H, N)) / np.sqrt(2 * H) / u[:, None])
    packed_w3 = pack_weight(n((K, N)) / np.sqrt(2 * K) / s)
    return {
        "x_words": packed_xT[0],
        "x_scales": packed_xT[1],
        "w1_words": packed_w1[0],
        "w1_scales": packed_w1[1],
        "sl": np.random.uniform(1.0, 2.0, (H, 1)).astype(np.float32),
        "th": (0.5 * n((H, 1))).astype(np.float32),
        "gn": (np.random.uniform(0.5, 1.5, (H, 1)) * u[:, None]).astype(np.float32),
        "w2_words": packed_w2[0],
        "w2_scales": packed_w2[1],
        "w3_words": packed_w3[0],
        "w3_scales": packed_w3[1],
        "offs": striped(np.random.permutation(T)[:S]),
        "n1": striped(np.random.permutation(S)),
        "n2": striped(np.random.permutation(S)),
        "hz": striped8(np.random.randint(0, T, (8, S))),
        "n3": striped8(np.stack([np.random.permutation(S) for _ in range(8)])),
        "n4": striped8(np.stack([np.random.permutation(S) for _ in range(8)])),
        "n5": striped8(np.stack([np.random.permutation(S) for _ in range(8)])),
    }


def reference(x_words, x_scales, w1_words, w1_scales, sl, th, gn, w2_words, w2_scales, w3_words, w3_scales, offs, n1, n2, hz, n3, n4, n5):
    xq = unpack_weight(x_words, x_scales)[:, unstriped(offs)]
    y = unpack_weight(w1_words, w1_scales).T @ xq
    st = y - y[:, unstriped(n1)]
    sg = sigmoid(f64(sl) * (st[:, unstriped(n2)] - f64(th)))
    z = f64(gn) * (y * sg)
    x_hz = unpack_weight(x_words, x_scales)[np.arange(K)[:, None], runs(hz, K)]
    h = unpack_weight(w2_words, w2_scales).T @ mxq(z, 0, "e4m3") + unpack_weight(w3_words, w3_scales).T @ x_hz
    out_0 = h + h[np.arange(N)[:, None], runs(n3, N)] - (np.maximum(h[np.arange(N)[:, None], runs(n4, N)], h[np.arange(N)[:, None], runs(n5, N)]))
    return (out_0,) + planes(out_0)

@@ -1,0 +1,271 @@
+from contextlib import ExitStack
+
+import concourse.mybir as mybir
+
+K, T, S, N, H = 512, 2048, 512, 512, 512
+FLOPS = 2 * S * (K * H + H * N + K * N)
+
+F32 = mybir.dt.float32
+BF16 = mybir.dt.bfloat16
+I32 = mybir.dt.int32
+U32 = mybir.dt.uint32
+U16 = mybir.dt.uint16
+U8 = mybir.dt.uint8
+FP8X4 = mybir.dt.float8_e4m3fn_x4
+ALU = mybir.AluOpType
+ACT = mybir.ActivationFunctionType
+
+P = 128
+PACK = 4
+HALF = S // 2
+HALVES = ((0, HALF), (HALF, S))
+Z_PIECES = ((0, 256), (256, 384), (384, 512))
+OUT_PIECES = ((0, 256), (256, 384), (384, 512))
+N5_ON_VECTOR = 1
+FUSED_N3 = 256
+
+
+def tile_picked_mixhehqtrim_none_po_kernel(
+    tc, x_words, x_scales, w1_words, w1_scales, sl, th, gn, w2_words, w2_scales, w3_words, w3_scales,
+    offs, n1, n2, hz, n3, n4, n5, out_0, out_1, out_2,
+):
+    nc = tc.nc
+
+    def words_view(words):
+        return words[0].rearrange("p c r -> p (c r)").bitcast(I32)
+
+    def entries(lst, a, b):
+        return lst[:, a // 16 : b // 16]
+
+    with ExitStack() as ctx:
+        lists = ctx.enter_context(tc.tile_pool(name="lists", bufs=1))
+        sb = ctx.enter_context(tc.tile_pool(name="sb", bufs=1))
+        psum = ctx.enter_context(tc.psum_pool(name="psum", bufs=1))
+
+        def tile(name, shape, dtype):
+            return sb.tile(shape, dtype, name=name, align_bytes=64)
+
+        def load_list(name, src):
+            lst = lists.tile([P, S // 16], U16, name=name)
+            nc.sync.dma_start(lst[:], src)
+            return lst
+
+        def load_scale_rows(plane, scales, first, queues=(nc.sync,) * 4):
+            for q, queue in enumerate(queues):
+                queue.dma_start(
+                    plane[32 * q + first : 32 * q + first + 4, :].bitcast(I32),
+                    scales[0, 4 * q : 4 * q + 4, :].bitcast(I32),
+                )
+
+        def load_rows(name, src):
+            col = tile(name, [P, PACK], F32)
+            nc.sync.dma_start(col[:], src.rearrange("(p t) o -> p (t o)", t=PACK))
+            return col
+
+        xs_win = tile("xs_win", [P, T], U8)
+        w1s_raw = tile("w1s_raw", [P, H], U8)
+        hs_win = tile("hs_win", [P, T], U8)
+        w32s_raw = tile("w32s_raw", [P, N], U8)
+        hs_plane = tile("hs_plane", [P, S], U8)
+        nc.gpsimd.memset(w1s_raw[:].bitcast(I32), 0)
+        for plane in (xs_win, hs_win, w32s_raw, hs_plane):
+            nc.vector.memset(plane[:].bitcast(I32), 0)
+
+        xw_win = tile("xw_win", [P, T], U32)
+        w1w_raw = tile("w1w_raw", [P, H], U32)
+        w3w_raw = tile("w3w_raw", [P, N], U32)
+        w2w_raw = tile("w2w_raw", [P, N], U32)
+        offs_t = load_list("offs_t", offs)
+        nc.scalar.dma_start(xw_win[:].bitcast(I32), words_view(x_words))
+        nc.sync.dma_start(w1w_raw[:].bitcast(I32), words_view(w1_words))
+        load_scale_rows(xs_win, x_scales, 0)
+        load_scale_rows(w1s_raw, w1_scales, 0, (nc.sync, nc.sync, nc.gpsimd, nc.gpsimd))
+        n1_t = load_list("n1_t", n1)
+        hz_t = load_list("hz_t", hz)
+        for e in range(2):
+            nc.sync.dma_start(hs_win[e:P:16, :].bitcast(I32), x_scales[0, e:16:2, :].bitcast(I32))
+        gn_t = load_rows("gn_t", gn)
+        sl_t = load_rows("sl_t", sl)
+        th_t = load_rows("th_t", th)
+        n2_t = load_list("n2_t", n2)
+        nc.sync.dma_start(w3w_raw[:].bitcast(I32), words_view(w3_words))
+        nc.sync.dma_start(w2w_raw[:].bitcast(I32), words_view(w2_words))
+        load_scale_rows(w32s_raw, w3_scales, 0)
+        load_scale_rows(w32s_raw, w2_scales, 4)
+        n4_t = load_list("n4_t", n4)
+        n5_t = load_list("n5_t", n5)
+        n3_t = load_list("n3_t", n3)
+
+        xq_s = tile("xq_s", [P, S], U8)
+        nc.vector.tensor_copy(xq_s[:], xs_win[:].indirect(offs_t[:]))
+        w1s = tile("w1s", [P, H], U8)
+        nc.vector.tensor_copy(
+            w1s[:].rearrange("p (t m) -> p t m", t=PACK), w1s_raw[:].rearrange("p (m t) -> p t m", t=PACK)
+        )
+        xq_w = []
+        for i, (a, b) in enumerate(HALVES):
+            g = tile(f"xq_w{i}", [P, HALF], U32)
+            nc.vector.tensor_copy(g[:], xw_win[:].indirect(entries(offs_t, a, b)))
+            xq_w.append(g)
+        w1w = []
+        for t in range(PACK):
+            w = tile(f"w1w{t}", [P, P], U32)
+            nc.scalar.copy(w[:], w1w_raw[:, t:H:PACK])
+            w1w.append(w)
+
+        y_ps = {}
+        y = [tile(f"y{t}", [P, S], F32) for t in range(PACK)]
+        for t in range(PACK):
+            for i, (a, b) in enumerate(HALVES):
+                acc = psum.tile([P, HALF], F32, name=f"yacc{t}{i}", tag=f"bank{2 * t + i}")
+                nc.tensor.matmul_mx(
+                    acc[:], lhsT=w1w[t][:].bitcast(FP8X4), lhsT_scale=w1s[:, t * P : (t + 1) * P],
+                    rhs=xq_w[i][:].bitcast(FP8X4), rhs_scale=xq_s[:, a:b], start=True, stop=True,
+                )
+                y_ps[t, i] = acc
+                if t == 0:
+                    nc.scalar.copy(y[t][:, a:b], acc[:])
+                else:
+                    nc.vector.tensor_copy(y[t][:, a:b], acc[:])
+
+        hs_got = tile("hs_got", [P, S], U8)
+        nc.vector.tensor_copy(hs_got[:], hs_win[:].indirect(hz_t[:]))
+        for r in range(4):
+            src = 16 * (r // 2) + r % 2
+            nc.sync.dma_start(hs_plane[r:P:32, :].bitcast(I32), hs_got[src:P:32, :].bitcast(I32))
+        xh_w = tile("xh_w", [P, S], U32)
+        nc.vector.tensor_copy(xh_w[:], xw_win[:].indirect(hz_t[:]))
+
+        bias = tile("bias", [P, PACK], F32)
+        nc.vector.scalar_tensor_tensor(bias[:], sl_t[:], -1.0, th_t[:], ALU.mult, ALU.mult)
+
+        st = [tile(f"st{t}", [P, S], F32) for t in range(PACK)]
+        yg = tile("yg", [P, PACK, S], F32)
+        for t in range(PACK):
+            for i, (a, b) in enumerate(HALVES):
+                g1 = tile(f"g1_{t}{i}", [P, HALF], F32)
+                nc.scalar.activation(g1[:], y[t][:].indirect(entries(n1_t, a, b)), ACT.Copy)
+                nc.vector.tensor_tensor(st[t][:, a:b], y_ps[t, i][:], g1[:], ALU.subtract)
+            nc.gpsimd.tensor_scalar(yg[:, t, :], y[t][:], gn_t[:, t : t + 1], 0.0, ALU.mult, ALU.add)
+
+        w3w = tile("w3w", [P, N], U32)
+        w2w = tile("w2w", [P, N], U32)
+        w32s = tile("w32s", [P, N], U8)
+        for dealt, raw in ((w3w, w3w_raw), (w32s, w32s_raw), (w2w, w2w_raw)):
+            nc.gpsimd.tensor_copy(
+                dealt[:].rearrange("p (t m) -> p t m", t=PACK), raw[:].rearrange("p (m t) -> p t m", t=PACK)
+            )
+
+        late = Z_PIECES[-1][0]
+        h_early = [psum.tile([P, late], F32, name=f"hearly{t}", tag=f"bank{2 * t}") for t in range(PACK)]
+        h_late = [psum.tile([P, S - late], F32, name=f"hlate{t}", tag=f"bank{2 * t + 1}") for t in range(PACK)]
+
+        def h_acc(t, a, b):
+            return h_early[t][:, a:b] if a < late else h_late[t][:, a - late : b - late]
+
+        for a, b in Z_PIECES:
+            for t in range(PACK):
+                cols = slice(t * P, (t + 1) * P)
+                nc.tensor.matmul_mx(
+                    h_acc(t, a, b), lhsT=w3w[:, cols].bitcast(FP8X4), lhsT_scale=w32s[:, cols],
+                    rhs=xh_w[:, a:b].bitcast(FP8X4), rhs_scale=hs_plane[:, a:b],
+                    start=a in (0, late), stop=False,
+                )
+
+        h = [tile(f"h{t}", [P, S], F32) for t in range(PACK)]
+        for a, b in Z_PIECES:
+            w = b - a
+            sg = tile(f"sg{a}", [P, PACK, w], F32)
+            for t in range(PACK):
+                nc.scalar.activation(
+                    sg[:, t, :], st[t][:].indirect(entries(n2_t, a, b)), ACT.Sigmoid,
+                    bias=bias[:, t : t + 1], scale=sl_t[:, t : t + 1],
+                )
+            zb = tile(f"zb{a}", [P, w, PACK], BF16)
+            nc.vector.tensor_tensor(
+                zb[:].rearrange("p (c i) t -> p c t i", i=4),
+                yg[:, :, a:b].rearrange("p t (c i) -> p c t i", i=4),
+                sg[:].rearrange("p t (c i) -> p c t i", i=4),
+                ALU.mult,
+            )
+            zw = tile(f"zw{a}", [P, w], U32)
+            zs = tile(f"zs{a}", [P, w], U8)
+            nc.vector.quantize_mx(zw[:].bitcast(FP8X4), zs[:], zb[:].rearrange("p c t -> p (c t)"))
+            for t in range(PACK):
+                cols = slice(t * P, (t + 1) * P)
+                nc.tensor.matmul_mx(
+                    h_acc(t, a, b), lhsT=w2w[:, cols].bitcast(FP8X4), lhsT_scale=w32s[4:P, cols],
+                    rhs=zw[:].bitcast(FP8X4), rhs_scale=zs[:], start=False, stop=b in (late, S),
+                )
+            if b == late:
+                for t in range(PACK):
+                    nc.scalar.copy(h[t][:, :late], h_early[t][:])
+        for t in range(PACK):
+            if t == 0:
+                nc.scalar.copy(h[t][:, late:], h_late[t][:])
+            else:
+                nc.vector.tensor_copy(h[t][:, late:], h_late[t][:])
+
+        ow = tile("ow", [P, S], U32)
+        osc = tile("osc", [P, S], U8)
+        out_rows = out_0.rearrange("(p t) j -> p t j", t=PACK)
+        out_words = words_view(out_1)
+        steps = [(a, b, t) for a, b in OUT_PIECES for t in range(PACK)]
+        res = {a: tile(f"res{a}", [P, PACK, b - a], F32) for a, b in OUT_PIECES}
+        ob = {a: tile(f"ob{a}", [P, b - a, PACK], BF16) for a, b in OUT_PIECES}
+        top = {}
+        rest = {}
+
+        def larger(i):
+            a, b, t = steps[i]
+            if a >= FUSED_N3:
+                g3 = tile(f"g3_{i}", [P, b - a], F32)
+                nc.scalar.activation(g3[:], h[t][:].indirect(entries(n3_t, a, b)), ACT.Copy)
+                rest[i] = tile(f"rest{i}", [P, b - a], F32)
+                nc.vector.tensor_tensor(rest[i][:], h[t][:, a:b], g3[:], ALU.add)
+            g4 = tile(f"g4_{i}", [P, b - a], F32)
+            g5 = tile(f"g5_{i}", [P, b - a], F32)
+            nc.scalar.activation(g4[:], h[t][:].indirect(entries(n4_t, a, b)), ACT.Copy)
+            if i < N5_ON_VECTOR:
+                nc.vector.tensor_copy(g5[:], h[t][:].indirect(entries(n5_t, a, b)))
+            else:
+                nc.scalar.activation(g5[:], h[t][:].indirect(entries(n5_t, a, b)), ACT.Copy)
+            top[i] = tile(f"top{i}", [P, b - a], F32)
+            nc.vector.tensor_tensor(top[i][:], g4[:], g5[:], ALU.max)
+
+        def less(i):
+            a, b, t = steps[i]
+            if a < FUSED_N3:
+                rest[i] = tile(f"rest{i}", [P, b - a], F32)
+                nc.vector.tensor_tensor(rest[i][:], h[t][:, a:b], top[i][:], ALU.subtract)
+            else:
+                nc.vector.tensor_tensor(res[a][:, t, :], rest[i][:], top[i][:], ALU.subtract)
+
+        def plus(i):
+            a, b, t = steps[i]
+            if a < FUSED_N3:
+                nc.vector.tensor_tensor(res[a][:, t, :], h[t][:].indirect(entries(n3_t, a, b)), rest[i][:], ALU.add)
+            if t == PACK - 1:
+                nc.sync.dma_start(out_rows[:, :, a:b], res[a][:])
+
+        def rounded(i):
+            a, b, t = steps[i]
+            if t == PACK - 1:
+                ob_walk = ob[a][:].rearrange("p (c i) t -> p c t i", i=4)
+                res_walk = res[a][:].rearrange("p t (c i) -> p c t i", i=4)
+                nc.vector.tensor_copy(ob_walk, res_walk)
+
+        def quantised(i):
+            a, b, t = steps[i]
+            if t == PACK - 1:
+                nc.vector.quantize_mx(ow[:, a:b].bitcast(FP8X4), osc[:, a:b], ob[a][:].rearrange("p c t -> p (c t)"))
+                nc.sync.dma_start(out_words[:, a:b], ow[:, a:b].bitcast(I32))
+
+        stages = (larger, less, plus, rounded, quantised)
+        for i in range(len(steps) + len(stages) - 1):
+            for lag, stage in enumerate(stages):
+                if 0 <= i - lag < len(steps):
+                    stage(i - lag)
+        for q in range(4):
+            queue = nc.sync if q % 2 else nc.scalar
+            queue.dma_start(out_2[0, 4 * q : 4 * q + 4, :].bitcast(I32), osc[32 * q : 32 * q + 4, :].bitcast(I32))

@@ -22,7 +22,7 @@ HALVES = ((0, HALF), (HALF, S))
 Z_PIECES = ((0, 256), (256, 384), (384, 512))
 OUT_PIECES = ((0, 256), (256, 384), (384, 512))
 N5_ON_VECTOR = 1
-FUSED_N3 = 256
+FUSED_N3 = 384
 
 
 def tile_picked_mixhehqtrim_none_po_kernel(
@@ -42,8 +42,8 @@ def tile_picked_mixhehqtrim_none_po_kernel(
         sb = ctx.enter_context(tc.tile_pool(name="sb", bufs=1))
         psum = ctx.enter_context(tc.psum_pool(name="psum", bufs=1))
 
-        def tile(name, shape, dtype):
-            return sb.tile(shape, dtype, name=name, align_bytes=64)
+        def tile(name, shape, dtype, tag=None):
+            return sb.tile(shape, dtype, name=name, tag=tag or name, align_bytes=64)
 
         def load_list(name, src):
             lst = lists.tile([P, S // 16], U16, name=name)
@@ -67,8 +67,7 @@ def tile_picked_mixhehqtrim_none_po_kernel(
         hs_win = tile("hs_win", [P, T], U8)
         w32s_raw = tile("w32s_raw", [P, N], U8)
         hs_plane = tile("hs_plane", [P, S], U8)
-        nc.gpsimd.memset(w1s_raw[:].bitcast(I32), 0)
-        for plane in (xs_win, hs_win, w32s_raw, hs_plane):
+        for plane in (w1s_raw, xs_win, hs_win, w32s_raw, hs_plane):
             nc.vector.memset(plane[:].bitcast(I32), 0)
 
         xw_win = tile("xw_win", [P, T], U32)
@@ -76,22 +75,22 @@ def tile_picked_mixhehqtrim_none_po_kernel(
         w3w_raw = tile("w3w_raw", [P, N], U32)
         w2w_raw = tile("w2w_raw", [P, N], U32)
         offs_t = load_list("offs_t", offs)
-        nc.scalar.dma_start(xw_win[:].bitcast(I32), words_view(x_words))
-        nc.sync.dma_start(w1w_raw[:].bitcast(I32), words_view(w1_words))
-        load_scale_rows(xs_win, x_scales, 0)
+        nc.sync.dma_start(xw_win[:].bitcast(I32), words_view(x_words))
+        load_scale_rows(xs_win, x_scales, 0, (nc.scalar,) * 4)
         load_scale_rows(w1s_raw, w1_scales, 0, (nc.sync, nc.sync, nc.gpsimd, nc.gpsimd))
+        nc.sync.dma_start(w1w_raw[:].bitcast(I32), words_view(w1_words))
         n1_t = load_list("n1_t", n1)
         hz_t = load_list("hz_t", hz)
         for e in range(2):
             nc.sync.dma_start(hs_win[e:P:16, :].bitcast(I32), x_scales[0, e:16:2, :].bitcast(I32))
         gn_t = load_rows("gn_t", gn)
-        sl_t = load_rows("sl_t", sl)
-        th_t = load_rows("th_t", th)
-        n2_t = load_list("n2_t", n2)
         nc.sync.dma_start(w3w_raw[:].bitcast(I32), words_view(w3_words))
-        nc.sync.dma_start(w2w_raw[:].bitcast(I32), words_view(w2_words))
         load_scale_rows(w32s_raw, w3_scales, 0)
         load_scale_rows(w32s_raw, w2_scales, 4)
+        n2_t = load_list("n2_t", n2)
+        sl_t = load_rows("sl_t", sl)
+        th_t = load_rows("th_t", th)
+        nc.sync.dma_start(w2w_raw[:].bitcast(I32), words_view(w2_words))
         n4_t = load_list("n4_t", n4)
         n5_t = load_list("n5_t", n5)
         n3_t = load_list("n3_t", n3)
@@ -99,14 +98,15 @@ def tile_picked_mixhehqtrim_none_po_kernel(
         xq_s = tile("xq_s", [P, S], U8)
         nc.vector.tensor_copy(xq_s[:], xs_win[:].indirect(offs_t[:]))
         w1s = tile("w1s", [P, H], U8)
-        nc.vector.tensor_copy(
-            w1s[:].rearrange("p (t m) -> p t m", t=PACK), w1s_raw[:].rearrange("p (m t) -> p t m", t=PACK)
-        )
+        w1s_dealt = w1s[:].rearrange("p (t m) -> p t m", t=PACK)
+        w1s_given = w1s_raw[:].rearrange("p (m t) -> p t m", t=PACK)
         xq_w = []
         for i, (a, b) in enumerate(HALVES):
-            g = tile(f"xq_w{i}", [P, HALF], U32)
+            g = tile(f"xq_w{i}", [P, HALF], U32, tag="xs_win" if i == 0 else None)
             nc.vector.tensor_copy(g[:], xw_win[:].indirect(entries(offs_t, a, b)))
             xq_w.append(g)
+            first = slice(0, 1) if i == 0 else slice(1, PACK)
+            nc.vector.tensor_copy(w1s_dealt[:, first, :], w1s_given[:, first, :])
         w1w = []
         for t in range(PACK):
             w = tile(f"w1w{t}", [P, P], U32)
@@ -133,28 +133,37 @@ def tile_picked_mixhehqtrim_none_po_kernel(
         for r in range(4):
             src = 16 * (r // 2) + r % 2
             nc.sync.dma_start(hs_plane[r:P:32, :].bitcast(I32), hs_got[src:P:32, :].bitcast(I32))
-        xh_w = tile("xh_w", [P, S], U32)
-        nc.vector.tensor_copy(xh_w[:], xw_win[:].indirect(hz_t[:]))
 
         bias = tile("bias", [P, PACK], F32)
         nc.vector.scalar_tensor_tensor(bias[:], sl_t[:], -1.0, th_t[:], ALU.mult, ALU.mult)
 
-        st = [tile(f"st{t}", [P, S], F32) for t in range(PACK)]
+        def deal(name, raw, dtype, tag=None):
+            dealt = tile(name, [P, N], dtype, tag=tag)
+            nc.vector.tensor_copy(
+                dealt[:].rearrange("p (t m) -> p t m", t=PACK), raw[:].rearrange("p (m t) -> p t m", t=PACK)
+            )
+            return dealt
+
         yg = tile("yg", [P, PACK, S], F32)
-        for t in range(PACK):
+        st = []
+
+        def subtract(t, tag=None):
+            st.append(tile(f"st{t}", [P, S], F32, tag=tag))
             for i, (a, b) in enumerate(HALVES):
                 g1 = tile(f"g1_{t}{i}", [P, HALF], F32)
                 nc.scalar.activation(g1[:], y[t][:].indirect(entries(n1_t, a, b)), ACT.Copy)
                 nc.vector.tensor_tensor(st[t][:, a:b], y_ps[t, i][:], g1[:], ALU.subtract)
             nc.gpsimd.tensor_scalar(yg[:, t, :], y[t][:], gn_t[:, t : t + 1], 0.0, ALU.mult, ALU.add)
 
-        w3w = tile("w3w", [P, N], U32)
-        w2w = tile("w2w", [P, N], U32)
-        w32s = tile("w32s", [P, N], U8)
-        for dealt, raw in ((w3w, w3w_raw), (w32s, w32s_raw), (w2w, w2w_raw)):
-            nc.gpsimd.tensor_copy(
-                dealt[:].rearrange("p (t m) -> p t m", t=PACK), raw[:].rearrange("p (m t) -> p t m", t=PACK)
-            )
+        subtract(0)
+        w3w = deal("w3w", w3w_raw, U32)
+        subtract(1, "w3w_raw")
+        subtract(2)
+        w32s = deal("w32s", w32s_raw, U8)
+        subtract(3, "w32s_raw")
+        xh_w = tile("xh_w", [P, S], U32, tag="g1_31")
+        nc.vector.tensor_copy(xh_w[:], xw_win[:].indirect(hz_t[:]))
+        w2w = deal("w2w", w2w_raw, U32, tag="g1_21")
 
         late = Z_PIECES[-1][0]
         h_early = [psum.tile([P, late], F32, name=f"hearly{t}", tag=f"bank{2 * t}") for t in range(PACK)]
@@ -173,19 +182,22 @@ def tile_picked_mixhehqtrim_none_po_kernel(
                 )
 
         h = [tile(f"h{t}", [P, S], F32) for t in range(PACK)]
+        sg_first = tile("sg_first", [P, PACK * HALF], F32)
+        sg_rest = tile("sg_rest", [P, PACK * HALF], F32, tag="g1_30")
         for a, b in Z_PIECES:
             w = b - a
-            sg = tile(f"sg{a}", [P, PACK, w], F32)
+            sg = sg_first[:] if a < HALF else sg_rest[:, PACK * (a - HALF) : PACK * (b - HALF)]
+            sg = sg.rearrange("p (t j) -> p t j", t=PACK)
             for t in range(PACK):
                 nc.scalar.activation(
                     sg[:, t, :], st[t][:].indirect(entries(n2_t, a, b)), ACT.Sigmoid,
                     bias=bias[:, t : t + 1], scale=sl_t[:, t : t + 1],
                 )
-            zb = tile(f"zb{a}", [P, w, PACK], BF16)
+            zb = tile(f"zb{a}", [P, w, PACK], BF16, tag="w2w_raw" if a == 0 else None)
             nc.vector.tensor_tensor(
                 zb[:].rearrange("p (c i) t -> p c t i", i=4),
                 yg[:, :, a:b].rearrange("p t (c i) -> p c t i", i=4),
-                sg[:].rearrange("p t (c i) -> p c t i", i=4),
+                sg.rearrange("p t (c i) -> p c t i", i=4),
                 ALU.mult,
             )
             zw = tile(f"zw{a}", [P, w], U32)

@@ -21,7 +21,7 @@ HALF = S // 2
 HALVES = ((0, HALF), (HALF, S))
 Z_PIECES = ((0, 256), (256, 384), (384, 512))
 OUT_PIECES = ((0, 256), (256, 384), (384, 512))
-N5_ON_VECTOR = 1
+N5_ON_VECTOR = 0
 FUSED_N3 = 384
 
 
@@ -70,6 +70,10 @@ def tile_picked_mixhehqtrim_none_po_kernel(
         for plane in (w1s_raw, xs_win, hs_win, w32s_raw, hs_plane):
             nc.vector.memset(plane[:].bitcast(I32), 0)
 
+        warm = tile("warm", [P, 2], F32)
+        nc.vector.memset(warm[:], 0.0)
+        warm_out = tile("warm_out", [P, 2], F32)
+        nc.scalar.activation(warm_out[:], warm[:], ACT.Sigmoid)
         xw_win = tile("xw_win", [P, T], U32)
         w1w_raw = tile("w1w_raw", [P, H], U32)
         w3w_raw = tile("w3w_raw", [P, N], U32)
@@ -83,13 +87,13 @@ def tile_picked_mixhehqtrim_none_po_kernel(
         hz_t = load_list("hz_t", hz)
         for e in range(2):
             nc.sync.dma_start(hs_win[e:P:16, :].bitcast(I32), x_scales[0, e:16:2, :].bitcast(I32))
-        gn_t = load_rows("gn_t", gn)
-        nc.sync.dma_start(w3w_raw[:].bitcast(I32), words_view(w3_words))
-        load_scale_rows(w32s_raw, w3_scales, 0)
-        load_scale_rows(w32s_raw, w2_scales, 4)
-        n2_t = load_list("n2_t", n2)
         sl_t = load_rows("sl_t", sl)
         th_t = load_rows("th_t", th)
+        gn_t = load_rows("gn_t", gn)
+        nc.sync.dma_start(w3w_raw[:].bitcast(I32), words_view(w3_words))
+        n2_t = load_list("n2_t", n2)
+        load_scale_rows(w32s_raw, w3_scales, 0)
+        load_scale_rows(w32s_raw, w2_scales, 4)
         nc.sync.dma_start(w2w_raw[:].bitcast(I32), words_view(w2_words))
         n4_t = load_list("n4_t", n4)
         n5_t = load_list("n5_t", n5)
@@ -135,11 +139,13 @@ def tile_picked_mixhehqtrim_none_po_kernel(
             nc.sync.dma_start(hs_plane[r:P:32, :].bitcast(I32), hs_got[src:P:32, :].bitcast(I32))
 
         bias = tile("bias", [P, PACK], F32)
-        nc.vector.scalar_tensor_tensor(bias[:], sl_t[:], -1.0, th_t[:], ALU.mult, ALU.mult)
+        sl_th = tile("sl_th", [P, PACK], F32)
+        nc.gpsimd.tensor_tensor(sl_th[:], sl_t[:], th_t[:], ALU.mult)
+        nc.gpsimd.tensor_scalar(bias[:], sl_th[:], -1.0, 0.0, ALU.mult, ALU.add)
 
-        def deal(name, raw, dtype, tag=None):
+        def deal(engine, name, raw, dtype, tag=None):
             dealt = tile(name, [P, N], dtype, tag=tag)
-            nc.vector.tensor_copy(
+            engine.tensor_copy(
                 dealt[:].rearrange("p (t m) -> p t m", t=PACK), raw[:].rearrange("p (m t) -> p t m", t=PACK)
             )
             return dealt
@@ -155,24 +161,22 @@ def tile_picked_mixhehqtrim_none_po_kernel(
                 nc.vector.tensor_tensor(st[t][:, a:b], y_ps[t, i][:], g1[:], ALU.subtract)
             nc.gpsimd.tensor_scalar(yg[:, t, :], y[t][:], gn_t[:, t : t + 1], 0.0, ALU.mult, ALU.add)
 
-        subtract(0)
-        w3w = deal("w3w", w3w_raw, U32)
-        subtract(1, "w3w_raw")
-        subtract(2)
-        w32s = deal("w32s", w32s_raw, U8)
-        subtract(3, "w32s_raw")
+        w3w = deal(nc.gpsimd, "w3w", w3w_raw, U32)
+        w32s = deal(nc.gpsimd, "w32s", w32s_raw, U8)
+        for t in range(PACK):
+            subtract(t, "hs_win" if t == 0 else None)
         xh_w = tile("xh_w", [P, S], U32, tag="g1_31")
         nc.vector.tensor_copy(xh_w[:], xw_win[:].indirect(hz_t[:]))
-        w2w = deal("w2w", w2w_raw, U32, tag="g1_21")
+        w2w = deal(nc.vector, "w2w", w2w_raw, U32, tag="xw_win")
 
-        late = Z_PIECES[-1][0]
+        late = HALF
         h_early = [psum.tile([P, late], F32, name=f"hearly{t}", tag=f"bank{2 * t}") for t in range(PACK)]
         h_late = [psum.tile([P, S - late], F32, name=f"hlate{t}", tag=f"bank{2 * t + 1}") for t in range(PACK)]
 
         def h_acc(t, a, b):
             return h_early[t][:, a:b] if a < late else h_late[t][:, a - late : b - late]
 
-        for a, b in Z_PIECES:
+        for a, b in HALVES:
             for t in range(PACK):
                 cols = slice(t * P, (t + 1) * P)
                 nc.tensor.matmul_mx(
@@ -181,28 +185,27 @@ def tile_picked_mixhehqtrim_none_po_kernel(
                     start=a in (0, late), stop=False,
                 )
 
-        h = [tile(f"h{t}", [P, S], F32) for t in range(PACK)]
-        sg_first = tile("sg_first", [P, PACK * HALF], F32)
-        sg_rest = tile("sg_rest", [P, PACK * HALF], F32, tag="g1_30")
-        for a, b in Z_PIECES:
+        h = [tile(f"h{t}", [P, S], F32, tag=slot) for t, slot in enumerate(("hs_win", "st1", "st2", "st3"))]
+        zb_all = tile("zb_all", [P, S * PACK], BF16, tag="w2w_raw")
+        sg_slots = ("g1_21", "g1_30", "g1_21")
+        for (a, b), slot in zip(Z_PIECES, sg_slots):
             w = b - a
-            sg = sg_first[:] if a < HALF else sg_rest[:, PACK * (a - HALF) : PACK * (b - HALF)]
-            sg = sg.rearrange("p (t j) -> p t j", t=PACK)
+            sg = tile(f"sg{a}", [P, PACK, w], F32, tag=slot)
             for t in range(PACK):
                 nc.scalar.activation(
                     sg[:, t, :], st[t][:].indirect(entries(n2_t, a, b)), ACT.Sigmoid,
                     bias=bias[:, t : t + 1], scale=sl_t[:, t : t + 1],
                 )
-            zb = tile(f"zb{a}", [P, w, PACK], BF16, tag="w2w_raw" if a == 0 else None)
+            zb = zb_all[:, PACK * a : PACK * b]
             nc.vector.tensor_tensor(
-                zb[:].rearrange("p (c i) t -> p c t i", i=4),
+                zb.rearrange("p (c i t) -> p c t i", i=4, t=PACK),
                 yg[:, :, a:b].rearrange("p t (c i) -> p c t i", i=4),
-                sg.rearrange("p t (c i) -> p c t i", i=4),
+                sg[:].rearrange("p t (c i) -> p c t i", i=4),
                 ALU.mult,
             )
             zw = tile(f"zw{a}", [P, w], U32)
             zs = tile(f"zs{a}", [P, w], U8)
-            nc.vector.quantize_mx(zw[:].bitcast(FP8X4), zs[:], zb[:].rearrange("p c t -> p (c t)"))
+            nc.vector.quantize_mx(zw[:].bitcast(FP8X4), zs[:], zb)
             for t in range(PACK):
                 cols = slice(t * P, (t + 1) * P)
                 nc.tensor.matmul_mx(

from contextlib import ExitStack

import concourse.mybir as mybir

K, T, S, N, H = 512, 2048, 512, 512, 512
FLOPS = 2 * S * (K * H + H * N + K * N)

F32 = mybir.dt.float32
BF16 = mybir.dt.bfloat16
I32 = mybir.dt.int32
U32 = mybir.dt.uint32
U16 = mybir.dt.uint16
U8 = mybir.dt.uint8
FP8X4 = mybir.dt.float8_e4m3fn_x4
ALU = mybir.AluOpType
ACT = mybir.ActivationFunctionType

P = 128
PACK = 4
HALF = S // 2
HALVES = ((0, HALF), (HALF, S))
Z_PIECES = ((0, 256), (256, 384), (384, 512))
OUT_PIECES = ((0, 256), (256, 384), (384, 512))
N5_ON_VECTOR = 0
FUSED_N3 = 384


def tile_picked_mixhehqtrim_none_po_kernel(
    tc, x_words, x_scales, w1_words, w1_scales, sl, th, gn, w2_words, w2_scales, w3_words, w3_scales,
    offs, n1, n2, hz, n3, n4, n5, out_0, out_1, out_2,
):
    nc = tc.nc

    def words_view(words):
        return words[0].rearrange("p c r -> p (c r)").bitcast(I32)

    def entries(lst, a, b):
        return lst[:, a // 16 : b // 16]

    with ExitStack() as ctx:
        lists = ctx.enter_context(tc.tile_pool(name="lists", bufs=1))
        sb = ctx.enter_context(tc.tile_pool(name="sb", bufs=1))
        psum = ctx.enter_context(tc.psum_pool(name="psum", bufs=1))

        def tile(name, shape, dtype, tag=None):
            return sb.tile(shape, dtype, name=name, tag=tag or name, align_bytes=64)

        def load_list(name, src):
            lst = lists.tile([P, S // 16], U16, name=name)
            nc.sync.dma_start(lst[:], src)
            return lst

        def load_scale_rows(plane, scales, first, queues=(nc.sync,) * 4):
            for q, queue in enumerate(queues):
                queue.dma_start(
                    plane[32 * q + first : 32 * q + first + 4, :].bitcast(I32),
                    scales[0, 4 * q : 4 * q + 4, :].bitcast(I32),
                )

        def load_rows(name, src):
            col = tile(name, [P, PACK], F32)
            nc.sync.dma_start(col[:], src.rearrange("(p t) o -> p (t o)", t=PACK))
            return col

        xs_win = tile("xs_win", [P, T], U8)
        w1s_raw = tile("w1s_raw", [P, H], U8)
        hs_win = tile("hs_win", [P, T], U8)
        w32s_raw = tile("w32s_raw", [P, N], U8)
        hs_plane = tile("hs_plane", [P, S], U8)
        for plane in (w1s_raw, xs_win, hs_win, w32s_raw, hs_plane):
            nc.vector.memset(plane[:].bitcast(I32), 0)

        warm = tile("warm", [P, 2], F32)
        nc.vector.memset(warm[:], 0.0)
        warm_out = tile("warm_out", [P, 2], F32)
        nc.scalar.activation(warm_out[:], warm[:], ACT.Sigmoid)
        xw_win = tile("xw_win", [P, T], U32)
        w1w_raw = tile("w1w_raw", [P, H], U32)
        w3w_raw = tile("w3w_raw", [P, N], U32)
        w2w_raw = tile("w2w_raw", [P, N], U32)
        offs_t = load_list("offs_t", offs)
        nc.sync.dma_start(xw_win[:].bitcast(I32), words_view(x_words))
        load_scale_rows(xs_win, x_scales, 0, (nc.scalar,) * 4)
        load_scale_rows(w1s_raw, w1_scales, 0, (nc.sync, nc.sync, nc.gpsimd, nc.gpsimd))
        nc.sync.dma_start(w1w_raw[:].bitcast(I32), words_view(w1_words))
        n1_t = load_list("n1_t", n1)
        hz_t = load_list("hz_t", hz)
        for e in range(2):
            nc.sync.dma_start(hs_win[e:P:16, :].bitcast(I32), x_scales[0, e:16:2, :].bitcast(I32))
        sl_t = load_rows("sl_t", sl)
        th_t = load_rows("th_t", th)
        gn_t = load_rows("gn_t", gn)
        nc.sync.dma_start(w3w_raw[:].bitcast(I32), words_view(w3_words))
        n2_t = load_list("n2_t", n2)
        load_scale_rows(w32s_raw, w3_scales, 0)
        load_scale_rows(w32s_raw, w2_scales, 4)
        nc.sync.dma_start(w2w_raw[:].bitcast(I32), words_view(w2_words))
        n4_t = load_list("n4_t", n4)
        n5_t = load_list("n5_t", n5)
        n3_t = load_list("n3_t", n3)

        xq_s = tile("xq_s", [P, S], U8)
        nc.vector.tensor_copy(xq_s[:], xs_win[:].indirect(offs_t[:]))
        w1s = tile("w1s", [P, H], U8)
        w1s_dealt = w1s[:].rearrange("p (t m) -> p t m", t=PACK)
        w1s_given = w1s_raw[:].rearrange("p (m t) -> p t m", t=PACK)
        xq_w = []
        for i, (a, b) in enumerate(HALVES):
            g = tile(f"xq_w{i}", [P, HALF], U32, tag="xs_win" if i == 0 else None)
            nc.vector.tensor_copy(g[:], xw_win[:].indirect(entries(offs_t, a, b)))
            xq_w.append(g)
            first = slice(0, 1) if i == 0 else slice(1, PACK)
            nc.vector.tensor_copy(w1s_dealt[:, first, :], w1s_given[:, first, :])
        w1w = []
        for t in range(PACK):
            w = tile(f"w1w{t}", [P, P], U32)
            nc.scalar.copy(w[:], w1w_raw[:, t:H:PACK])
            w1w.append(w)

        y_ps = {}
        y = [tile(f"y{t}", [P, S], F32) for t in range(PACK)]
        for t in range(PACK):
            for i, (a, b) in enumerate(HALVES):
                acc = psum.tile([P, HALF], F32, name=f"yacc{t}{i}", tag=f"bank{2 * t + i}")
                nc.tensor.matmul_mx(
                    acc[:], lhsT=w1w[t][:].bitcast(FP8X4), lhsT_scale=w1s[:, t * P : (t + 1) * P],
                    rhs=xq_w[i][:].bitcast(FP8X4), rhs_scale=xq_s[:, a:b], start=True, stop=True,
                )
                y_ps[t, i] = acc
                if t == 0:
                    nc.scalar.copy(y[t][:, a:b], acc[:])
                else:
                    nc.vector.tensor_copy(y[t][:, a:b], acc[:])

        hs_got = tile("hs_got", [P, S], U8)
        nc.vector.tensor_copy(hs_got[:], hs_win[:].indirect(hz_t[:]))
        for r in range(4):
            src = 16 * (r // 2) + r % 2
            nc.sync.dma_start(hs_plane[r:P:32, :].bitcast(I32), hs_got[src:P:32, :].bitcast(I32))

        bias = tile("bias", [P, PACK], F32)
        sl_th = tile("sl_th", [P, PACK], F32)
        nc.gpsimd.tensor_tensor(sl_th[:], sl_t[:], th_t[:], ALU.mult)
        nc.gpsimd.tensor_scalar(bias[:], sl_th[:], -1.0, 0.0, ALU.mult, ALU.add)

        def deal(engine, name, raw, dtype, tag=None):
            dealt = tile(name, [P, N], dtype, tag=tag)
            engine.tensor_copy(
                dealt[:].rearrange("p (t m) -> p t m", t=PACK), raw[:].rearrange("p (m t) -> p t m", t=PACK)
            )
            return dealt

        yg = tile("yg", [P, PACK, S], F32)
        st = []

        def subtract(t, tag=None):
            st.append(tile(f"st{t}", [P, S], F32, tag=tag))
            for i, (a, b) in enumerate(HALVES):
                g1 = tile(f"g1_{t}{i}", [P, HALF], F32)
                nc.scalar.activation(g1[:], y[t][:].indirect(entries(n1_t, a, b)), ACT.Copy)
                nc.vector.tensor_tensor(st[t][:, a:b], y_ps[t, i][:], g1[:], ALU.subtract)
            nc.gpsimd.tensor_scalar(yg[:, t, :], y[t][:], gn_t[:, t : t + 1], 0.0, ALU.mult, ALU.add)

        w3w = deal(nc.gpsimd, "w3w", w3w_raw, U32)
        w32s = deal(nc.gpsimd, "w32s", w32s_raw, U8)
        for t in range(PACK):
            subtract(t, "hs_win" if t == 0 else None)
        xh_w = tile("xh_w", [P, S], U32, tag="g1_31")
        nc.vector.tensor_copy(xh_w[:], xw_win[:].indirect(hz_t[:]))
        w2w = deal(nc.vector, "w2w", w2w_raw, U32, tag="xw_win")

        late = HALF
        h_early = [psum.tile([P, late], F32, name=f"hearly{t}", tag=f"bank{2 * t}") for t in range(PACK)]
        h_late = [psum.tile([P, S - late], F32, name=f"hlate{t}", tag=f"bank{2 * t + 1}") for t in range(PACK)]

        def h_acc(t, a, b):
            return h_early[t][:, a:b] if a < late else h_late[t][:, a - late : b - late]

        for a, b in HALVES:
            for t in range(PACK):
                cols = slice(t * P, (t + 1) * P)
                nc.tensor.matmul_mx(
                    h_acc(t, a, b), lhsT=w3w[:, cols].bitcast(FP8X4), lhsT_scale=w32s[:, cols],
                    rhs=xh_w[:, a:b].bitcast(FP8X4), rhs_scale=hs_plane[:, a:b],
                    start=a in (0, late), stop=False,
                )

        h = [tile(f"h{t}", [P, S], F32, tag=slot) for t, slot in enumerate(("hs_win", "st1", "st2", "st3"))]
        zb_all = tile("zb_all", [P, S * PACK], BF16, tag="w2w_raw")
        sg_slots = ("g1_21", "g1_30", "g1_21")
        for (a, b), slot in zip(Z_PIECES, sg_slots):
            w = b - a
            sg = tile(f"sg{a}", [P, PACK, w], F32, tag=slot)
            for t in range(PACK):
                nc.scalar.activation(
                    sg[:, t, :], st[t][:].indirect(entries(n2_t, a, b)), ACT.Sigmoid,
                    bias=bias[:, t : t + 1], scale=sl_t[:, t : t + 1],
                )
            zb = zb_all[:, PACK * a : PACK * b]
            nc.vector.tensor_tensor(
                zb.rearrange("p (c i t) -> p c t i", i=4, t=PACK),
                yg[:, :, a:b].rearrange("p t (c i) -> p c t i", i=4),
                sg[:].rearrange("p t (c i) -> p c t i", i=4),
                ALU.mult,
            )
            zw = tile(f"zw{a}", [P, w], U32)
            zs = tile(f"zs{a}", [P, w], U8)
            nc.vector.quantize_mx(zw[:].bitcast(FP8X4), zs[:], zb)
            for t in range(PACK):
                cols = slice(t * P, (t + 1) * P)
                nc.tensor.matmul_mx(
                    h_acc(t, a, b), lhsT=w2w[:, cols].bitcast(FP8X4), lhsT_scale=w32s[4:P, cols],
                    rhs=zw[:].bitcast(FP8X4), rhs_scale=zs[:], start=False, stop=b in (late, S),
                )
            if b == late:
                for t in range(PACK):
                    nc.scalar.copy(h[t][:, :late], h_early[t][:])
        for t in range(PACK):
            if t == 0:
                nc.scalar.copy(h[t][:, late:], h_late[t][:])
            else:
                nc.vector.tensor_copy(h[t][:, late:], h_late[t][:])

        ow = tile("ow", [P, S], U32)
        osc = tile("osc", [P, S], U8)
        out_rows = out_0.rearrange("(p t) j -> p t j", t=PACK)
        out_words = words_view(out_1)
        steps = [(a, b, t) for a, b in OUT_PIECES for t in range(PACK)]
        res = {a: tile(f"res{a}", [P, PACK, b - a], F32) for a, b in OUT_PIECES}
        ob = {a: tile(f"ob{a}", [P, b - a, PACK], BF16) for a, b in OUT_PIECES}
        top = {}
        rest = {}

        def larger(i):
            a, b, t = steps[i]
            if a >= FUSED_N3:
                g3 = tile(f"g3_{i}", [P, b - a], F32)
                nc.scalar.activation(g3[:], h[t][:].indirect(entries(n3_t, a, b)), ACT.Copy)
                rest[i] = tile(f"rest{i}", [P, b - a], F32)
                nc.vector.tensor_tensor(rest[i][:], h[t][:, a:b], g3[:], ALU.add)
            g4 = tile(f"g4_{i}", [P, b - a], F32)
            g5 = tile(f"g5_{i}", [P, b - a], F32)
            nc.scalar.activation(g4[:], h[t][:].indirect(entries(n4_t, a, b)), ACT.Copy)
            if i < N5_ON_VECTOR:
                nc.vector.tensor_copy(g5[:], h[t][:].indirect(entries(n5_t, a, b)))
            else:
                nc.scalar.activation(g5[:], h[t][:].indirect(entries(n5_t, a, b)), ACT.Copy)
            top[i] = tile(f"top{i}", [P, b - a], F32)
            nc.vector.tensor_tensor(top[i][:], g4[:], g5[:], ALU.max)

        def less(i):
            a, b, t = steps[i]
            if a < FUSED_N3:
                rest[i] = tile(f"rest{i}", [P, b - a], F32)
                nc.vector.tensor_tensor(rest[i][:], h[t][:, a:b], top[i][:], ALU.subtract)
            else:
                nc.vector.tensor_tensor(res[a][:, t, :], rest[i][:], top[i][:], ALU.subtract)

        def plus(i):
            a, b, t = steps[i]
            if a < FUSED_N3:
                nc.vector.tensor_tensor(res[a][:, t, :], h[t][:].indirect(entries(n3_t, a, b)), rest[i][:], ALU.add)
            if t == PACK - 1:
                nc.sync.dma_start(out_rows[:, :, a:b], res[a][:])

        def rounded(i):
            a, b, t = steps[i]
            if t == PACK - 1:
                ob_walk = ob[a][:].rearrange("p (c i) t -> p c t i", i=4)
                res_walk = res[a][:].rearrange("p t (c i) -> p c t i", i=4)
                nc.vector.tensor_copy(ob_walk, res_walk)

        def quantised(i):
            a, b, t = steps[i]
            if t == PACK - 1:
                nc.vector.quantize_mx(ow[:, a:b].bitcast(FP8X4), osc[:, a:b], ob[a][:].rearrange("p c t -> p (c t)"))
                nc.sync.dma_start(out_words[:, a:b], ow[:, a:b].bitcast(I32))

        stages = (larger, less, plus, rounded, quantised)
        for i in range(len(steps) + len(stages) - 1):
            for lag, stage in enumerate(stages):
                if 0 <= i - lag < len(steps):
                    stage(i - lag)
        for q in range(4):
            queue = nc.sync if q % 2 else nc.scalar
            queue.dma_start(out_2[0, 4 * q : 4 * q + 4, :].bitcast(I32), osc[32 * q : 32 * q + 4, :].bitcast(I32))
